import numpy as np
import ml_dtypes


def mxq(x, axis, fmt="e4m3"):
    dtype, down = {"e4m3": (ml_dtypes.float8_e4m3fn, 7), "e5m2": (ml_dtypes.float8_e5m2, 14)}[fmt]
    v = np.moveaxis(np.asarray(x, np.float32).astype(ml_dtypes.bfloat16).astype(np.float64), axis, -1)
    blocks = v.reshape(v.shape[:-1] + (-1, 32))
    amax = np.abs(blocks).max(-1, keepdims=True)
    byte = np.maximum(np.where(amax > 0, np.frexp(amax)[1] - 1 + 127, 0) - down, 1)
    scale = np.exp2(byte - 127.0)
    codes = (blocks / scale).astype(np.float32).astype(dtype).astype(np.float64)
    return np.moveaxis((codes * scale).reshape(v.shape), -1, axis)


WIDE = False


def mx_kscale(k):
    if not WIDE:
        return np.ones(k)
    levels = np.array([10, -10, 5, -5, 0])
    if k % 512:
        return np.exp2(np.random.permutation(np.resize(levels, k // 32))).repeat(32)
    a = np.empty((k // 512, 16))
    for p in range(k // 512):
        a[p, :8] = np.random.permutation(np.resize(levels, 8))
        for g in range(8):
            far = levels[np.abs(levels - a[p, g]) >= 10]
            a[p, g + 8] = far[np.random.randint(len(far))]
    return np.exp2(a.ravel()).repeat(32)


def f64(x):
    return np.asarray(x).astype(np.float64)


def striped(idx):
    return np.tile(idx.reshape(-1, 16).T, (8, 1)).astype(np.uint16)


def unstriped(offs):
    return offs[:16].T.reshape(-1).astype(np.int64)


E2M1 = np.array([0.0, 0.5, 1.0, 1.5, 2.0, 3.0, 4.0, 6.0, -0.0, -0.5, -1.0, -1.5, -2.0, -3.0, -4.0, -6.0])


def pack_weight(w, fmt):
    k, n = w.shape
    w = f64(np.asarray(w, np.float32).astype(ml_dtypes.bfloat16)).reshape(k // 32, 32, n)
    amax = np.abs(w).max(1)
    if fmt == "e4m3":
        byte = np.frexp(amax)[1] - 1 + 127 - 7
    else:
        mant, ex = np.frexp(amax / 6.0)
        byte = np.where(mant > 0.5, ex, ex - 1) + 127
    byte = np.clip(np.where(amax > 0, byte, 1), 1, 254)
    scaled = (w * np.exp2(127.0 - byte)[:, None, :]).reshape(k, n).astype(np.float32)
    by_word = np.ascontiguousarray(scaled.reshape(k // 512, 128, 4, n).transpose(0, 1, 3, 2))
    if fmt == "e4m3":
        words = by_word.astype(ml_dtypes.float8_e4m3fn).view(np.uint8)
    else:
        c = by_word.astype(ml_dtypes.float4_e2m1fn).view(np.uint8) & 0xF
        words = (c[..., 0::2] | (c[..., 1::2] << 4)).reshape(k // 512, 128, 2 * n)
    return np.ascontiguousarray(words), np.ascontiguousarray(byte.astype(np.uint8).reshape(k // 512, 16, n))


def unpack_weight(words, scales, fmt):
    g, _, n = scales.shape
    words = np.ascontiguousarray(words).reshape(g, 128, n, -1)
    if fmt == "e4m3":
        vals = words.view(ml_dtypes.float8_e4m3fn).astype(np.float64)
    else:
        nib = np.empty((g, 128, n, 4), np.uint8)
        nib[..., 0::2] = words & 0xF
        nib[..., 1::2] = words >> 4
        vals = E2M1[nib]
    vals = vals * np.repeat(np.exp2(scales.astype(np.float64) - 127.0), 8, axis=1)[..., None]
    return vals.transpose(0, 1, 3, 2).reshape(g * 512, n)


def gelu(v):
    return 0.5 * v * (1.0 + np.tanh(np.sqrt(2.0 / np.pi) * (v + 0.044715 * v**3)))


K, T, H, S, S2, T3, P = 1536, 2048, 512, 1024, 512, 2048, 512

def setup_inputs():
    n = np.random.standard_normal
    s = mx_kscale(K)[:, None]
    u = mx_kscale(H)[:, None]
    tab_words, tab_scales = pack_weight(n((K, T)) * s, "e4m3")
    tab2_words, tab2_scales = pack_weight(n((H, T3)) / np.sqrt(H) / u, "e4m3")
    w4_words, w4_scales = pack_weight(1.5 * n((K, H)) / np.sqrt(K) / s, "e2m1")
    return {
        "tab_words": tab_words, "tab_scales": tab_scales,
        "offs": striped(np.random.permutation(T)[:S]),
        "w4_words": w4_words, "w4_scales": w4_scales,
        "gain": (np.random.uniform(0.5, 1.3, H) * u[:, 0]).astype(np.float32),
        "w1": (n((K, H)) / np.sqrt(K) / s * u.T).astype(np.float32),
        "b1": (0.5 * n(H) * u[:, 0]).astype(np.float32),
        "tab2_words": tab2_words, "tab2_scales": tab2_scales,
        "offs2": striped(np.random.permutation(T3)[:S2]),
        "w2": (0.85 * n((H, S2)) / np.sqrt(H) / u).astype(np.float32),
        "sev": np.random.uniform(0.6, 3.0, S2).astype(np.float32),
        "thr": n(S2).astype(np.float32),
        "prior": (0.4 * n((S2, P))).astype(np.float32),
        "pos1": striped(np.random.permutation(S)[:P]),
        "pos2": striped(np.random.permutation(S)[:P]),
    }

def reference(tab_words, tab_scales, offs, w4_words, w4_scales, gain, w1, b1, tab2_words, tab2_scales, offs2, w2, sev, thr, prior, pos1, pos2):
    v = unpack_weight(tab_words, tab_scales, "e4m3")[:, unstriped(offs)]
    v2 = unpack_weight(tab2_words, tab2_scales, "e4m3")[:, unstriped(offs2)]
    w4 = unpack_weight(w4_words, w4_scales, "e2m1")
    z = w4.T @ v
    h = z / (1.0 + np.exp(-z)) * f64(gain)[:, None]
    g = (mxq(f64(w1), 0, "e4m3").T @ v) + f64(b1)[:, None]
    match = v2.T @ mxq(h, 0, "e4m3")
    docket = mxq(f64(w2), 0, "e4m3").T @ mxq(g, 0, "e4m3")
    e = match * docket
    a = 1.0 / (1.0 + np.exp(-(f64(sev)[:, None] * e[:, unstriped(pos1)] + f64(thr)[:, None])))
    return a - f64(prior) + e[:, unstriped(pos2)]

@@ -1,0 +1,281 @@
+from contextlib import ExitStack
+
+import concourse.mybir as mybir
+
+K, T, H, S, S2, T3, NP = 1536, 2048, 512, 1024, 512, 2048, 512
+FLOPS = 2 * (2 * K * H * S + 2 * H * S2 * S)
+
+F32 = mybir.dt.float32
+BF16 = mybir.dt.bfloat16
+I32 = mybir.dt.int32
+U32 = mybir.dt.uint32
+U16 = mybir.dt.uint16
+U8 = mybir.dt.uint8
+FP8X4 = mybir.dt.float8_e4m3fn_x4
+FP4X4 = mybir.dt.float4_e2m1fn_x4
+ACT = mybir.ActivationFunctionType
+ALU = mybir.AluOpType
+
+P = 128
+PACK = 4
+PASSES = K // (P * PACK)
+HALF = 512
+HALVES = S // HALF
+CHUNK = 256
+SCALE_SPAN = 100
+
+
+def tile_list_duty_complaint_triage_kernel(
+    tc, tab_words, tab_scales, offs, w4_words, w4_scales, gain, w1, b1, tab2_words, tab2_scales,
+    offs2, w2, sev, thr, prior, pos1, pos2, out,
+):
+    nc = tc.nc
+    with ExitStack() as ctx:
+        keep = ctx.enter_context(tc.tile_pool(name="keep", bufs=1))
+        ring = ctx.enter_context(tc.tile_pool(name="ring", bufs=4))
+        psum = ctx.enter_context(tc.psum_pool(name="psum", bufs=1))
+
+        def held(name, shape, dtype):
+            return keep.tile(shape, dtype, name=name, align_bytes=64)
+
+        def bank(index, shape):
+            return psum.tile(shape, F32, name="bank%d" % index)
+
+        offs_sb = keep.tile([P, S // 16], U16, name="offs_sb")
+        offs2_sb = keep.tile([P, S2 // 16], U16, name="offs2_sb")
+        pos1_sb = keep.tile([P, NP // 16], U16, name="pos1_sb")
+        pos2_sb = keep.tile([P, NP // 16], U16, name="pos2_sb")
+
+        tab_sb = [held("tab%d" % a, [P, T], U32) for a in range(PASSES)]
+        tabsc_sb = held("tabsc", [P, T], U8)
+        tab2_sb = held("tabB", [P, T3], U32)
+        tab2sc_sb = held("tabBsc", [P, T3], U8)
+        w4_raw = held("w4_raw", [P, PASSES * H], U16)
+        w4sc_raw = held("w4sc_raw", [P, PASSES * H], U8)
+        w1_raw = [held("w1_raw%d" % a, [P, PACK, H], F32) for a in range(PASSES)]
+        w2_raw = held("w2_raw", [P, PACK, S2], F32)
+        prior_sb = held("prior_sb", [P, 4, NP], F32)
+        gain_sb = held("gain_sb", [P, PACK], F32)
+        b1_sb = held("b1_sb", [P, PACK], F32)
+        sev_sb = held("sev_sb", [P, 4], F32)
+        thr_sb = held("thr_sb", [P, 4], F32)
+        v_scales = [held("v_scales%d" % a, [P, S], U8) for a in range(PASSES)]
+
+        def load_words(tile, words):
+            nc.sync.dma_start(out=tile[:].bitcast(I32), in_=words.rearrange("p n i -> p (n i)").bitcast(I32))
+
+        def load_rows(tile, rows):
+            nc.sync.dma_start(out=tile[:], in_=rows.rearrange("(p j) c -> p j c", j=PACK))
+
+        nc.vector.memset(tabsc_sb[:].bitcast(I32), 0)
+        nc.gpsimd.memset(w4sc_raw[:].bitcast(I32), 0)
+        nc.sync.dma_start(offs_sb[:], offs)
+        load_words(tab_sb[0], tab_words[0])
+        for q in range(4):
+            nc.scalar.dma_start(
+                out=tabsc_sb[32 * q : 32 * q + 4 * PASSES, :].bitcast(I32),
+                in_=tab_scales[:, 4 * q : 4 * q + 4, :].bitcast(I32),
+            )
+        for q in range(4):
+            nc.gpsimd.dma_start(
+                out=w4sc_raw[32 * q : 32 * q + 4, :].bitcast(I32).rearrange("r (a c) -> r a c", a=PASSES),
+                in_=w4_scales[:, 4 * q : 4 * q + 4, :].bitcast(I32).rearrange("a r c -> r a c"),
+            )
+        nc.sync.dma_start(
+            out=w4_raw[:].bitcast(I32).rearrange("p (a c) -> p a c", a=PASSES),
+            in_=w4_words.bitcast(I32).rearrange("a p c -> p a c"),
+        )
+        load_rows(w1_raw[0], w1[0:512, :])
+        load_words(tab_sb[1], tab_words[1])
+        load_words(tab_sb[2], tab_words[2])
+        nc.sync.dma_start(out=gain_sb[:], in_=gain.rearrange("(p t) -> p t", t=PACK))
+        load_rows(w1_raw[1], w1[512:1024, :])
+        load_rows(w1_raw[2], w1[1024:1536, :])
+        for a in range(1, PASSES):
+            nc.vector.memset(v_scales[a][:].bitcast(I32), 0)
+        nc.vector.memset(tab2sc_sb[:].bitcast(I32), 0)
+        nc.sync.dma_start(offs2_sb[:], offs2)
+        for q in range(4):
+            nc.sync.dma_start(
+                out=tab2sc_sb[32 * q : 32 * q + 4, :].bitcast(I32),
+                in_=tab2_scales[0, 4 * q : 4 * q + 4, :].bitcast(I32),
+            )
+        load_words(tab2_sb, tab2_words[0])
+        nc.sync.dma_start(out=b1_sb[:], in_=b1.rearrange("(p t) -> p t", t=PACK))
+        load_rows(w2_raw, w2)
+        nc.sync.dma_start(pos1_sb[:], pos1)
+        nc.sync.dma_start(pos2_sb[:], pos2)
+        with nc.allow_non_contiguous_dma(reason="one value a partition"):
+            nc.sync.dma_start(out=sev_sb[:], in_=sev.rearrange("(c p) -> p c", p=P))
+            nc.sync.dma_start(out=thr_sb[:], in_=thr.rearrange("(c p) -> p c", p=P))
+        nc.sync.dma_start(out=prior_sb[:], in_=prior.rearrange("(c p) n -> p c n", p=P))
+
+        w4_codes = held("w4_codes", [P, PASSES * H], U16)
+        w4_sc = held("w4_sc", [P, PASSES * H], U8)
+        for a in range(PASSES):
+            nc.gpsimd.tensor_copy(
+                out=w4_sc[:, a * H : (a + 1) * H].rearrange("p (t m) -> p t m", t=PACK),
+                in_=w4sc_raw[:, a * H : (a + 1) * H].rearrange("p (m t) -> p t m", t=PACK),
+            )
+        nc.scalar.copy(
+            out=w4_codes[:].rearrange("p (a t m) -> p a t m", a=PASSES, t=PACK),
+            in_=w4_raw[:].rearrange("p (a m t) -> p a t m", a=PASSES, t=PACK),
+        )
+
+        v_words = [held("v_words%d" % a, [P, S], U32) for a in range(PASSES)]
+        nc.vector.tensor_copy(v_words[0][:], tab_sb[0][:].indirect(offs_sb[:]))
+        nc.vector.tensor_copy(v_scales[0][:], tabsc_sb[:].indirect(offs_sb[:]))
+        for a in range(1, PASSES):
+            nc.scalar.dma_start(
+                out=v_scales[a][0:SCALE_SPAN, :].bitcast(I32),
+                in_=v_scales[0][4 * a : 4 * a + SCALE_SPAN, :].bitcast(I32),
+            )
+        nc.vector.tensor_copy(v_words[1][:], tab_sb[1][:].indirect(offs_sb[:]))
+        for hf in range(HALVES):
+            nc.vector.tensor_copy(
+                v_words[2][:, hf * HALF : (hf + 1) * HALF],
+                tab_sb[2][:].indirect(offs_sb[:, hf * HALF // 16 : (hf + 1) * HALF // 16]),
+            )
+
+        w1_bf = [held("w1_bf%d" % a, [P, PACK * H], BF16) for a in range(PASSES)]
+        w1_codes = [held("w1_codes%d" % a, [P, H], U32) for a in range(PASSES)]
+        w1_sc = [held("w1_sc%d" % a, [P, H], U8) for a in range(PASSES)]
+
+        def round_w1(a, copy):
+            copy(
+                out=w1_bf[a][:].rearrange("p (t m j) -> p m j t", t=PACK, j=PACK),
+                in_=w1_raw[a][:].rearrange("p j (m t) -> p m j t", t=PACK),
+            )
+
+        def quantize(codes, scales, values):
+            nc.vector.quantize_mx(out=codes.bitcast(FP8X4), scales=scales, in_=values)
+
+        round_w1(0, nc.scalar.copy)
+
+        z_banks = [[bank(hf * PACK + t, [P, HALF]) for t in range(PACK)] for hf in range(HALVES)]
+        for a in range(PASSES):
+            for hf in range(HALVES):
+                cols = slice(hf * HALF, (hf + 1) * HALF)
+                for t in range(PACK):
+                    wcols = slice(a * H + t * P, a * H + (t + 1) * P)
+                    nc.tensor.matmul_mx(
+                        out=z_banks[hf][t][:],
+                        lhsT=w4_codes[:, wcols].bitcast(FP4X4),
+                        lhsT_scale=w4_sc[:, wcols],
+                        rhs=v_words[a][:, cols].bitcast(FP8X4),
+                        rhs_scale=v_scales[a][:, cols],
+                        start=(a == 0),
+                        stop=(a == PASSES - 1),
+                    )
+
+        quantize(w1_codes[0][:], w1_sc[0][:], w1_bf[0][:])
+        round_w1(1, nc.vector.tensor_copy)
+        quantize(w1_codes[1][:], w1_sc[1][:], w1_bf[1][:])
+
+        h_bf = [held("h_bf%d" % hf, [P, HALF * PACK], BF16) for hf in range(HALVES)]
+        h_codes = held("h_codes", [P, S], U32)
+        h_sc = held("h_sc", [P, S], U8)
+        for hf in range(HALVES):
+            for part in range(HALF // CHUNK):
+                silu = ring.tile([P, PACK, CHUNK], F32, name="silu")
+                for t in range(PACK):
+                    nc.scalar.activation(
+                        out=silu[:, t, :], in_=z_banks[hf][t][:, part * CHUNK : (part + 1) * CHUNK], func=ACT.Silu
+                    )
+                nc.vector.tensor_tensor(
+                    out=h_bf[hf][:, part * CHUNK * PACK : (part + 1) * CHUNK * PACK].rearrange(
+                        "p (c i t) -> p c t i", i=4, t=PACK
+                    ),
+                    in0=silu[:].rearrange("p t (c i) -> p c t i", i=4),
+                    in1=gain_sb[:].unsqueeze(1).unsqueeze(3).to_broadcast([P, CHUNK // 4, PACK, 4]),
+                    op=ALU.mult,
+                )
+            cols = slice(hf * HALF, (hf + 1) * HALF)
+            quantize(h_codes[:, cols], h_sc[:, cols], h_bf[hf][:])
+
+        round_w1(2, nc.scalar.copy)
+        quantize(w1_codes[2][:], w1_sc[2][:], w1_bf[2][:])
+
+        g_banks = [[bank(hf * PACK + t, [P, HALF]) for t in range(PACK)] for hf in range(HALVES)]
+        for a in range(PASSES):
+            for hf in range(HALVES):
+                cols = slice(hf * HALF, (hf + 1) * HALF)
+                for t in range(PACK):
+                    wcols = slice(t * P, (t + 1) * P)
+                    nc.tensor.matmul_mx(
+                        out=g_banks[hf][t][:],
+                        lhsT=w1_codes[a][:, wcols].bitcast(FP8X4),
+                        lhsT_scale=w1_sc[a][:, wcols],
+                        rhs=v_words[a][:, cols].bitcast(FP8X4),
+                        rhs_scale=v_scales[a][:, cols],
+                        start=(a == 0),
+                        stop=(a == PASSES - 1),
+                    )
+
+        v2_words = held("v2_words", [P, S2], U32)
+        v2_sc = held("v2_sc", [P, S2], U8)
+        nc.vector.tensor_copy(v2_words[:], tab2_sb[:].indirect(offs2_sb[:]))
+        nc.vector.tensor_copy(v2_sc[:], tab2sc_sb[:].indirect(offs2_sb[:]))
+
+        w2_bf = held("w2_bf", [P, PACK * S2], BF16)
+        w2_codes = held("w2_codes", [P, S2], U32)
+        w2_sc = held("w2_sc", [P, S2], U8)
+        nc.scalar.copy(
+            out=w2_bf[:].rearrange("p (c i j) -> p c j i", i=4, j=PACK),
+            in_=w2_raw[:].rearrange("p j (c i) -> p c j i", i=4),
+        )
+        quantize(w2_codes[:], w2_sc[:], w2_bf[:])
+
+        g_codes = held("g_codes", [P, S], U32)
+        g_sc = held("g_sc", [P, S], U8)
+        for hf in range(HALVES):
+            g_rows = held("g_rows%d" % hf, [P, PACK, HALF], BF16)
+            g_bf = held("g_bf%d" % hf, [P, HALF * PACK], BF16)
+            for t in range(PACK):
+                nc.scalar.activation(
+                    out=g_rows[:, t, :], in_=g_banks[hf][t][:], func=ACT.Identity, bias=b1_sb[:, t : t + 1]
+                )
+            nc.vector.tensor_copy(
+                out=g_bf[:].rearrange("p (c i t) -> p c t i", i=4, t=PACK),
+                in_=g_rows[:].rearrange("p t (c i) -> p c t i", i=4),
+            )
+            cols = slice(hf * HALF, (hf + 1) * HALF)
+            quantize(g_codes[:, cols], g_sc[:, cols], g_bf[:])
+
+        e_sb = [held("e%d" % m, [P, S], F32) for m in range(4)]
+        match_sb = {}
+        for hf in range(HALVES):
+            cols = slice(hf * HALF, (hf + 1) * HALF)
+            for m in range(4):
+                rows = slice(m * P, (m + 1) * P)
+                acc = bank(hf * 4 + m, [P, HALF])
+                nc.tensor.matmul_mx(
+                    out=acc[:], lhsT=v2_words[:, rows].bitcast(FP8X4), lhsT_scale=v2_sc[:, rows],
+                    rhs=h_codes[:, cols].bitcast(FP8X4), rhs_scale=h_sc[:, cols], start=True, stop=True,
+                )
+                match_sb[hf, m] = held("match%d_%d" % (hf, m), [P, HALF], F32)
+                nc.scalar.copy(out=match_sb[hf, m][:], in_=acc[:])
+
+        def score(hf, m):
+            cols = slice(hf * HALF, (hf + 1) * HALF)
+            rows = slice(m * P, (m + 1) * P)
+            acc = bank(hf * 4 + m, [P, HALF])
+            nc.tensor.matmul_mx(
+                out=acc[:], lhsT=w2_codes[:, rows].bitcast(FP8X4), lhsT_scale=w2_sc[:, rows],
+                rhs=g_codes[:, cols].bitcast(FP8X4), rhs_scale=g_sc[:, cols], start=True, stop=True,
+            )
+            nc.vector.tensor_tensor(out=e_sb[m][:, cols], in0=acc[:], in1=match_sb[hf, m][:], op=ALU.mult)
+
+        for m in range(4):
+            score(0, m)
+        for m in range(4):
+            score(1, m)
+            look = ring.tile([P, NP], F32, name="look")
+            nc.scalar.activation(
+                out=look[:], in_=e_sb[m][:].indirect(pos1_sb[:]), func=ACT.Sigmoid,
+                bias=thr_sb[:, m : m + 1], scale=sev_sb[:, m : m + 1],
+            )
+            pick = ring.tile([P, NP], F32, name="pick")
+            nc.vector.tensor_tensor(pick[:], e_sb[m][:].indirect(pos2_sb[:]), prior_sb[:, m, :], ALU.subtract)
+            nc.vector.tensor_tensor(out=look[:], in0=look[:], in1=pick[:], op=ALU.add)
+            nc.sync.dma_start(out=out[m * P : (m + 1) * P, :], in_=look[:])

@@ -1,4 +1,5 @@
 from contextlib import ExitStack
+from itertools import product
 
 import concourse.mybir as mybir
 
@@ -21,7 +22,6 @@ PACK = 4
 PASSES = K // (P * PACK)
 HALF = 512
 HALVES = S // HALF
-CHUNK = 256
 SCALE_SPAN = 100
 
 
@@ -59,7 +59,6 @@ def tile_list_duty_complaint_triage_kernel(
         b1_sb = held("b1_sb", [P, PACK], F32)
         sev_sb = held("sev_sb", [P, 4], F32)
         thr_sb = held("thr_sb", [P, 4], F32)
-        v_scales = [held("v_scales%d" % a, [P, S], U8) for a in range(PASSES)]
 
         def load_words(tile, words):
             nc.sync.dma_start(out=tile[:].bitcast(I32), in_=words.rearrange("p n i -> p (n i)").bitcast(I32))
@@ -71,38 +70,36 @@ def tile_list_duty_complaint_triage_kernel(
         nc.gpsimd.memset(w4sc_raw[:].bitcast(I32), 0)
         nc.sync.dma_start(offs_sb[:], offs)
         load_words(tab_sb[0], tab_words[0])
+        nc.sync.dma_start(
+            out=w4_raw[:].bitcast(I32).rearrange("p (a c) -> p a c", a=PASSES),
+            in_=w4_words.bitcast(I32).rearrange("a p c -> p a c"),
+        )
         for q in range(4):
-            nc.scalar.dma_start(
+            nc.sync.dma_start(
                 out=tabsc_sb[32 * q : 32 * q + 4 * PASSES, :].bitcast(I32),
                 in_=tab_scales[:, 4 * q : 4 * q + 4, :].bitcast(I32),
             )
+        load_words(tab_sb[1], tab_words[1])
         for q in range(4):
             nc.gpsimd.dma_start(
                 out=w4sc_raw[32 * q : 32 * q + 4, :].bitcast(I32).rearrange("r (a c) -> r a c", a=PASSES),
                 in_=w4_scales[:, 4 * q : 4 * q + 4, :].bitcast(I32).rearrange("a r c -> r a c"),
             )
-        nc.sync.dma_start(
-            out=w4_raw[:].bitcast(I32).rearrange("p (a c) -> p a c", a=PASSES),
-            in_=w4_words.bitcast(I32).rearrange("a p c -> p a c"),
-        )
         load_rows(w1_raw[0], w1[0:512, :])
-        load_words(tab_sb[1], tab_words[1])
         load_words(tab_sb[2], tab_words[2])
-        nc.sync.dma_start(out=gain_sb[:], in_=gain.rearrange("(p t) -> p t", t=PACK))
         load_rows(w1_raw[1], w1[512:1024, :])
         load_rows(w1_raw[2], w1[1024:1536, :])
-        for a in range(1, PASSES):
-            nc.vector.memset(v_scales[a][:].bitcast(I32), 0)
+        nc.sync.dma_start(out=gain_sb[:], in_=gain.rearrange("(p t) -> p t", t=PACK))
         nc.vector.memset(tab2sc_sb[:].bitcast(I32), 0)
+        load_rows(w2_raw, w2)
         nc.sync.dma_start(offs2_sb[:], offs2)
+        load_words(tab2_sb, tab2_words[0])
         for q in range(4):
             nc.sync.dma_start(
                 out=tab2sc_sb[32 * q : 32 * q + 4, :].bitcast(I32),
                 in_=tab2_scales[0, 4 * q : 4 * q + 4, :].bitcast(I32),
             )
-        load_words(tab2_sb, tab2_words[0])
         nc.sync.dma_start(out=b1_sb[:], in_=b1.rearrange("(p t) -> p t", t=PACK))
-        load_rows(w2_raw, w2)
         nc.sync.dma_start(pos1_sb[:], pos1)
         nc.sync.dma_start(pos2_sb[:], pos2)
         with nc.allow_non_contiguous_dma(reason="one value a partition"):
@@ -112,30 +109,39 @@ def tile_list_duty_complaint_triage_kernel(
 
         w4_codes = held("w4_codes", [P, PASSES * H], U16)
         w4_sc = held("w4_sc", [P, PASSES * H], U8)
-        for a in range(PASSES):
-            nc.gpsimd.tensor_copy(
-                out=w4_sc[:, a * H : (a + 1) * H].rearrange("p (t m) -> p t m", t=PACK),
-                in_=w4sc_raw[:, a * H : (a + 1) * H].rearrange("p (m t) -> p t m", t=PACK),
-            )
         nc.scalar.copy(
             out=w4_codes[:].rearrange("p (a t m) -> p a t m", a=PASSES, t=PACK),
             in_=w4_raw[:].rearrange("p (a m t) -> p a t m", a=PASSES, t=PACK),
         )
 
+        for a in range(PASSES):
+            nc.gpsimd.tensor_copy(
+                out=w4_sc[:, a * H : (a + 1) * H].rearrange("p (t m) -> p t m", t=PACK),
+                in_=w4sc_raw[:, a * H : (a + 1) * H].rearrange("p (m t) -> p t m", t=PACK),
+            )
+
         v_words = [held("v_words%d" % a, [P, S], U32) for a in range(PASSES)]
+
+        v_packed = held("v_packed", [P, S], U8)
+        v_moved = held("w4_raw", [P, (PASSES - 1) * S], U8)
+        v_scales = [v_packed[:]] + [v_moved[:, a * S : (a + 1) * S] for a in range(PASSES - 1)]
+
+        def gather_half(picked, table, hf):
+            nc.vector.tensor_copy(
+                picked[:, hf * HALF : (hf + 1) * HALF],
+                table[:].indirect(offs_sb[:, hf * HALF // 16 : (hf + 1) * HALF // 16]),
+            )
+
         nc.vector.tensor_copy(v_words[0][:], tab_sb[0][:].indirect(offs_sb[:]))
-        nc.vector.tensor_copy(v_scales[0][:], tabsc_sb[:].indirect(offs_sb[:]))
+        nc.vector.tensor_copy(v_packed[:], tabsc_sb[:].indirect(offs_sb[:]))
         for a in range(1, PASSES):
             nc.scalar.dma_start(
                 out=v_scales[a][0:SCALE_SPAN, :].bitcast(I32),
-                in_=v_scales[0][4 * a : 4 * a + SCALE_SPAN, :].bitcast(I32),
+                in_=v_packed[4 * a : 4 * a + SCALE_SPAN, :].bitcast(I32),
             )
-        nc.vector.tensor_copy(v_words[1][:], tab_sb[1][:].indirect(offs_sb[:]))
-        for hf in range(HALVES):
-            nc.vector.tensor_copy(
-                v_words[2][:, hf * HALF : (hf + 1) * HALF],
-                tab_sb[2][:].indirect(offs_sb[:, hf * HALF // 16 : (hf + 1) * HALF // 16]),
-            )
+        for a in range(1, PASSES):
+            for hf in range(HALVES):
+                gather_half(v_words[a], tab_sb[a], hf)
 
         w1_bf = [held("w1_bf%d" % a, [P, PACK * H], BF16) for a in range(PASSES)]
         w1_codes = [held("w1_codes%d" % a, [P, H], U32) for a in range(PASSES)]
@@ -150,11 +156,10 @@ def tile_list_duty_complaint_triage_kernel(
         def quantize(codes, scales, values):
             nc.vector.quantize_mx(out=codes.bitcast(FP8X4), scales=scales, in_=values)
 
-        round_w1(0, nc.scalar.copy)
 
         z_banks = [[bank(hf * PACK + t, [P, HALF]) for t in range(PACK)] for hf in range(HALVES)]
-        for a in range(PASSES):
-            for hf in range(HALVES):
+        for a, hf in sorted(product(range(PASSES), range(HALVES)), key=lambda step: step[0] + 1.5 * step[1]):
+            if True:
                 cols = slice(hf * HALF, (hf + 1) * HALF)
                 for t in range(PACK):
                     wcols = slice(a * H + t * P, a * H + (t + 1) * P)
@@ -168,54 +173,56 @@ def tile_list_duty_complaint_triage_kernel(
                         stop=(a == PASSES - 1),
                     )
 
-        quantize(w1_codes[0][:], w1_sc[0][:], w1_bf[0][:])
+        round_w1(0, nc.scalar.copy)
         round_w1(1, nc.vector.tensor_copy)
+        quantize(w1_codes[0][:], w1_sc[0][:], w1_bf[0][:])
         quantize(w1_codes[1][:], w1_sc[1][:], w1_bf[1][:])
-
-        h_bf = [held("h_bf%d" % hf, [P, HALF * PACK], BF16) for hf in range(HALVES)]
-        h_codes = held("h_codes", [P, S], U32)
-        h_sc = held("h_sc", [P, S], U8)
-        for hf in range(HALVES):
-            for part in range(HALF // CHUNK):
-                silu = ring.tile([P, PACK, CHUNK], F32, name="silu")
-                for t in range(PACK):
-                    nc.scalar.activation(
-                        out=silu[:, t, :], in_=z_banks[hf][t][:, part * CHUNK : (part + 1) * CHUNK], func=ACT.Silu
-                    )
-                nc.vector.tensor_tensor(
-                    out=h_bf[hf][:, part * CHUNK * PACK : (part + 1) * CHUNK * PACK].rearrange(
-                        "p (c i t) -> p c t i", i=4, t=PACK
-                    ),
-                    in0=silu[:].rearrange("p t (c i) -> p c t i", i=4),
-                    in1=gain_sb[:].unsqueeze(1).unsqueeze(3).to_broadcast([P, CHUNK // 4, PACK, 4]),
-                    op=ALU.mult,
-                )
-            cols = slice(hf * HALF, (hf + 1) * HALF)
-            quantize(h_codes[:, cols], h_sc[:, cols], h_bf[hf][:])
-
-        round_w1(2, nc.scalar.copy)
+        round_w1(2, nc.vector.tensor_copy)
         quantize(w1_codes[2][:], w1_sc[2][:], w1_bf[2][:])
 
-        g_banks = [[bank(hf * PACK + t, [P, HALF]) for t in range(PACK)] for hf in range(HALVES)]
-        for a in range(PASSES):
-            for hf in range(HALVES):
-                cols = slice(hf * HALF, (hf + 1) * HALF)
-                for t in range(PACK):
-                    wcols = slice(t * P, (t + 1) * P)
-                    nc.tensor.matmul_mx(
-                        out=g_banks[hf][t][:],
-                        lhsT=w1_codes[a][:, wcols].bitcast(FP8X4),
-                        lhsT_scale=w1_sc[a][:, wcols],
-                        rhs=v_words[a][:, cols].bitcast(FP8X4),
-                        rhs_scale=v_scales[a][:, cols],
-                        start=(a == 0),
-                        stop=(a == PASSES - 1),
-                    )
+        h_codes = held("h_codes", [P, S], U32)
+        h_sc = held("h_sc", [P, S], U8)
+        silu = [held(name, [P, PACK, HALF], F32) for name in ("silu0", "silu1")]
+        for hf in range(HALVES):
+            for t in range(PACK):
+                nc.scalar.activation(out=silu[hf][:, t, :], in_=z_banks[hf][t][:], func=ACT.Silu)
+
+        def scale_h(hf, buffer):
+            h_bf = held(buffer, [P, HALF * PACK], BF16)
+            nc.vector.tensor_tensor(
+                out=h_bf[:].rearrange("p (c i t) -> p c t i", i=4, t=PACK),
+                in0=silu[hf][:].rearrange("p t (c i) -> p c t i", i=4),
+                in1=gain_sb[:].unsqueeze(1).unsqueeze(3).to_broadcast([P, HALF // 4, PACK, 4]),
+                op=ALU.mult,
+            )
+            return h_bf
+
+        h_bf = scale_h(0, "w1_raw2")
+        quantize(h_codes[:, :HALF], h_sc[:, :HALF], h_bf[:])
+        h_bf = scale_h(1, "w1_bf2")
 
         v2_words = held("v2_words", [P, S2], U32)
         v2_sc = held("v2_sc", [P, S2], U8)
         nc.vector.tensor_copy(v2_words[:], tab2_sb[:].indirect(offs2_sb[:]))
+        quantize(h_codes[:, HALF:], h_sc[:, HALF:], h_bf[:])
         nc.vector.tensor_copy(v2_sc[:], tab2sc_sb[:].indirect(offs2_sb[:]))
+
+        g_banks = [[bank(hf * PACK + t, [P, HALF]) for t in range(PACK)] for hf in range(HALVES)]
+        if True:
+            for hf in range(HALVES):
+                cols = slice(hf * HALF, (hf + 1) * HALF)
+                for a in range(PASSES):
+                    for t in range(PACK):
+                        wcols = slice(t * P, (t + 1) * P)
+                        nc.tensor.matmul_mx(
+                            out=g_banks[hf][t][:],
+                            lhsT=w1_codes[a][:, wcols].bitcast(FP8X4),
+                            lhsT_scale=w1_sc[a][:, wcols],
+                            rhs=v_words[a][:, cols].bitcast(FP8X4),
+                            rhs_scale=v_scales[a][:, cols],
+                            start=(a == 0),
+                            stop=(a == PASSES - 1),
+                        )
 
         w2_bf = held("w2_bf", [P, PACK * S2], BF16)
         w2_codes = held("w2_codes", [P, S2], U32)
@@ -248,7 +255,7 @@ def tile_list_duty_complaint_triage_kernel(
             cols = slice(hf * HALF, (hf + 1) * HALF)
             for m in range(4):
                 rows = slice(m * P, (m + 1) * P)
-                acc = bank(hf * 4 + m, [P, HALF])
+                acc = bank(4 + m, [P, HALF])
                 nc.tensor.matmul_mx(
                     out=acc[:], lhsT=v2_words[:, rows].bitcast(FP8X4), lhsT_scale=v2_sc[:, rows],
                     rhs=h_codes[:, cols].bitcast(FP8X4), rhs_scale=h_sc[:, cols], start=True, stop=True,
@@ -259,23 +266,35 @@ def tile_list_duty_complaint_triage_kernel(
         def score(hf, m):
             cols = slice(hf * HALF, (hf + 1) * HALF)
             rows = slice(m * P, (m + 1) * P)
-            acc = bank(hf * 4 + m, [P, HALF])
+            acc = bank(m, [P, HALF])
             nc.tensor.matmul_mx(
                 out=acc[:], lhsT=w2_codes[:, rows].bitcast(FP8X4), lhsT_scale=w2_sc[:, rows],
                 rhs=g_codes[:, cols].bitcast(FP8X4), rhs_scale=g_sc[:, cols], start=True, stop=True,
             )
             nc.vector.tensor_tensor(out=e_sb[m][:, cols], in0=acc[:], in1=match_sb[hf, m][:], op=ALU.mult)
 
-        for m in range(4):
-            score(0, m)
-        for m in range(4):
-            score(1, m)
-            look = ring.tile([P, NP], F32, name="look")
+        for hf in range(HALVES):
+            for m in range(4):
+                score(hf, m)
+
+        looks, picks = {}, {}
+
+        def fetch(m):
+            looks[m] = ring.tile([P, NP], F32, name="look")
             nc.scalar.activation(
-                out=look[:], in_=e_sb[m][:].indirect(pos1_sb[:]), func=ACT.Sigmoid,
+                out=looks[m][:], in_=e_sb[m][:].indirect(pos1_sb[:]), func=ACT.Sigmoid,
                 bias=thr_sb[:, m : m + 1], scale=sev_sb[:, m : m + 1],
             )
-            pick = ring.tile([P, NP], F32, name="pick")
-            nc.vector.tensor_tensor(pick[:], e_sb[m][:].indirect(pos2_sb[:]), prior_sb[:, m, :], ALU.subtract)
-            nc.vector.tensor_tensor(out=look[:], in0=look[:], in1=pick[:], op=ALU.add)
-            nc.sync.dma_start(out=out[m * P : (m + 1) * P, :], in_=look[:])
+            picks[m] = ring.tile([P, NP], F32, name="pick")
+            nc.vector.tensor_tensor(picks[m][:], e_sb[m][:].indirect(pos2_sb[:]), prior_sb[:, m, :], ALU.subtract)
+
+        def finish(m, cols):
+            nc.vector.tensor_tensor(out=looks[m][:, cols], in0=looks[m][:, cols], in1=picks[m][:, cols], op=ALU.add)
+            nc.sync.dma_start(out=out[m * P : (m + 1) * P, cols], in_=looks[m][:, cols])
+
+        fetch(0)
+        for m in range(1, 4):
+            fetch(m)
+            finish(m - 1, slice(0, NP))
+        finish(3, slice(0, NP // 2))
+        finish(3, slice(NP // 2, NP))

from contextlib import ExitStack
from itertools import product

import concourse.mybir as mybir

K, T, H, S, S2, T3, NP = 1536, 2048, 512, 1024, 512, 2048, 512
FLOPS = 2 * (2 * K * H * S + 2 * H * S2 * S)

F32 = mybir.dt.float32
BF16 = mybir.dt.bfloat16
I32 = mybir.dt.int32
U32 = mybir.dt.uint32
U16 = mybir.dt.uint16
U8 = mybir.dt.uint8
FP8X4 = mybir.dt.float8_e4m3fn_x4
FP4X4 = mybir.dt.float4_e2m1fn_x4
ACT = mybir.ActivationFunctionType
ALU = mybir.AluOpType

P = 128
PACK = 4
PASSES = K // (P * PACK)
HALF = 512
HALVES = S // HALF
SCALE_SPAN = 100


def tile_list_duty_complaint_triage_kernel(
    tc, tab_words, tab_scales, offs, w4_words, w4_scales, gain, w1, b1, tab2_words, tab2_scales,
    offs2, w2, sev, thr, prior, pos1, pos2, out,
):
    nc = tc.nc
    with ExitStack() as ctx:
        keep = ctx.enter_context(tc.tile_pool(name="keep", bufs=1))
        ring = ctx.enter_context(tc.tile_pool(name="ring", bufs=4))
        psum = ctx.enter_context(tc.psum_pool(name="psum", bufs=1))

        def held(name, shape, dtype):
            return keep.tile(shape, dtype, name=name, align_bytes=64)

        def bank(index, shape):
            return psum.tile(shape, F32, name="bank%d" % index)

        offs_sb = keep.tile([P, S // 16], U16, name="offs_sb")
        offs2_sb = keep.tile([P, S2 // 16], U16, name="offs2_sb")
        pos1_sb = keep.tile([P, NP // 16], U16, name="pos1_sb")
        pos2_sb = keep.tile([P, NP // 16], U16, name="pos2_sb")

        tab_sb = [held("tab%d" % a, [P, T], U32) for a in range(PASSES)]
        tabsc_sb = held("tabsc", [P, T], U8)
        tab2_sb = held("tabB", [P, T3], U32)
        tab2sc_sb = held("tabBsc", [P, T3], U8)
        w4_raw = held("w4_raw", [P, PASSES * H], U16)
        w4sc_raw = held("w4sc_raw", [P, PASSES * H], U8)
        w1_raw = [held("w1_raw%d" % a, [P, PACK, H], F32) for a in range(PASSES)]
        w2_raw = held("w2_raw", [P, PACK, S2], F32)
        prior_sb = held("prior_sb", [P, 4, NP], F32)
        gain_sb = held("gain_sb", [P, PACK], F32)
        b1_sb = held("b1_sb", [P, PACK], F32)
        sev_sb = held("sev_sb", [P, 4], F32)
        thr_sb = held("thr_sb", [P, 4], F32)

        def load_words(tile, words):
            nc.sync.dma_start(out=tile[:].bitcast(I32), in_=words.rearrange("p n i -> p (n i)").bitcast(I32))

        def load_rows(tile, rows):
            nc.sync.dma_start(out=tile[:], in_=rows.rearrange("(p j) c -> p j c", j=PACK))

        nc.vector.memset(tabsc_sb[:].bitcast(I32), 0)
        nc.gpsimd.memset(w4sc_raw[:].bitcast(I32), 0)
        nc.sync.dma_start(offs_sb[:], offs)
        load_words(tab_sb[0], tab_words[0])
        nc.sync.dma_start(
            out=w4_raw[:].bitcast(I32).rearrange("p (a c) -> p a c", a=PASSES),
            in_=w4_words.bitcast(I32).rearrange("a p c -> p a c"),
        )
        for q in range(4):
            nc.sync.dma_start(
                out=tabsc_sb[32 * q : 32 * q + 4 * PASSES, :].bitcast(I32),
                in_=tab_scales[:, 4 * q : 4 * q + 4, :].bitcast(I32),
            )
        load_words(tab_sb[1], tab_words[1])
        for q in range(4):
            nc.gpsimd.dma_start(
                out=w4sc_raw[32 * q : 32 * q + 4, :].bitcast(I32).rearrange("r (a c) -> r a c", a=PASSES),
                in_=w4_scales[:, 4 * q : 4 * q + 4, :].bitcast(I32).rearrange("a r c -> r a c"),
            )
        load_rows(w1_raw[0], w1[0:512, :])
        load_words(tab_sb[2], tab_words[2])
        load_rows(w1_raw[1], w1[512:1024, :])
        load_rows(w1_raw[2], w1[1024:1536, :])
        nc.sync.dma_start(out=gain_sb[:], in_=gain.rearrange("(p t) -> p t", t=PACK))
        nc.vector.memset(tab2sc_sb[:].bitcast(I32), 0)
        load_rows(w2_raw, w2)
        nc.sync.dma_start(offs2_sb[:], offs2)
        load_words(tab2_sb, tab2_words[0])
        for q in range(4):
            nc.sync.dma_start(
                out=tab2sc_sb[32 * q : 32 * q + 4, :].bitcast(I32),
                in_=tab2_scales[0, 4 * q : 4 * q + 4, :].bitcast(I32),
            )
        nc.sync.dma_start(out=b1_sb[:], in_=b1.rearrange("(p t) -> p t", t=PACK))
        nc.sync.dma_start(pos1_sb[:], pos1)
        nc.sync.dma_start(pos2_sb[:], pos2)
        with nc.allow_non_contiguous_dma(reason="one value a partition"):
            nc.sync.dma_start(out=sev_sb[:], in_=sev.rearrange("(c p) -> p c", p=P))
            nc.sync.dma_start(out=thr_sb[:], in_=thr.rearrange("(c p) -> p c", p=P))
        nc.sync.dma_start(out=prior_sb[:], in_=prior.rearrange("(c p) n -> p c n", p=P))

        w4_codes = held("w4_codes", [P, PASSES * H], U16)
        w4_sc = held("w4_sc", [P, PASSES * H], U8)
        nc.scalar.copy(
            out=w4_codes[:].rearrange("p (a t m) -> p a t m", a=PASSES, t=PACK),
            in_=w4_raw[:].rearrange("p (a m t) -> p a t m", a=PASSES, t=PACK),
        )

        for a in range(PASSES):
            nc.gpsimd.tensor_copy(
                out=w4_sc[:, a * H : (a + 1) * H].rearrange("p (t m) -> p t m", t=PACK),
                in_=w4sc_raw[:, a * H : (a + 1) * H].rearrange("p (m t) -> p t m", t=PACK),
            )

        v_words = [held("v_words%d" % a, [P, S], U32) for a in range(PASSES)]

        v_packed = held("v_packed", [P, S], U8)
        v_moved = held("w4_raw", [P, (PASSES - 1) * S], U8)
        v_scales = [v_packed[:]] + [v_moved[:, a * S : (a + 1) * S] for a in range(PASSES - 1)]

        def gather_half(picked, table, hf):
            nc.vector.tensor_copy(
                picked[:, hf * HALF : (hf + 1) * HALF],
                table[:].indirect(offs_sb[:, hf * HALF // 16 : (hf + 1) * HALF // 16]),
            )

        nc.vector.tensor_copy(v_words[0][:], tab_sb[0][:].indirect(offs_sb[:]))
        nc.vector.tensor_copy(v_packed[:], tabsc_sb[:].indirect(offs_sb[:]))
        for a in range(1, PASSES):
            nc.scalar.dma_start(
                out=v_scales[a][0:SCALE_SPAN, :].bitcast(I32),
                in_=v_packed[4 * a : 4 * a + SCALE_SPAN, :].bitcast(I32),
            )
        for a in range(1, PASSES):
            for hf in range(HALVES):
                gather_half(v_words[a], tab_sb[a], hf)

        w1_bf = [held("w1_bf%d" % a, [P, PACK * H], BF16) for a in range(PASSES)]
        w1_codes = [held("w1_codes%d" % a, [P, H], U32) for a in range(PASSES)]
        w1_sc = [held("w1_sc%d" % a, [P, H], U8) for a in range(PASSES)]

        def round_w1(a, copy):
            copy(
                out=w1_bf[a][:].rearrange("p (t m j) -> p m j t", t=PACK, j=PACK),
                in_=w1_raw[a][:].rearrange("p j (m t) -> p m j t", t=PACK),
            )

        def quantize(codes, scales, values):
            nc.vector.quantize_mx(out=codes.bitcast(FP8X4), scales=scales, in_=values)


        z_banks = [[bank(hf * PACK + t, [P, HALF]) for t in range(PACK)] for hf in range(HALVES)]
        for a, hf in sorted(product(range(PASSES), range(HALVES)), key=lambda step: step[0] + 1.5 * step[1]):
            if True:
                cols = slice(hf * HALF, (hf + 1) * HALF)
                for t in range(PACK):
                    wcols = slice(a * H + t * P, a * H + (t + 1) * P)
                    nc.tensor.matmul_mx(
                        out=z_banks[hf][t][:],
                        lhsT=w4_codes[:, wcols].bitcast(FP4X4),
                        lhsT_scale=w4_sc[:, wcols],
                        rhs=v_words[a][:, cols].bitcast(FP8X4),
                        rhs_scale=v_scales[a][:, cols],
                        start=(a == 0),
                        stop=(a == PASSES - 1),
                    )

        round_w1(0, nc.scalar.copy)
        round_w1(1, nc.vector.tensor_copy)
        quantize(w1_codes[0][:], w1_sc[0][:], w1_bf[0][:])
        quantize(w1_codes[1][:], w1_sc[1][:], w1_bf[1][:])
        round_w1(2, nc.vector.tensor_copy)
        quantize(w1_codes[2][:], w1_sc[2][:], w1_bf[2][:])

        h_codes = held("h_codes", [P, S], U32)
        h_sc = held("h_sc", [P, S], U8)
        silu = [held(name, [P, PACK, HALF], F32) for name in ("silu0", "silu1")]
        for hf in range(HALVES):
            for t in range(PACK):
                nc.scalar.activation(out=silu[hf][:, t, :], in_=z_banks[hf][t][:], func=ACT.Silu)

        def scale_h(hf, buffer):
            h_bf = held(buffer, [P, HALF * PACK], BF16)
            nc.vector.tensor_tensor(
                out=h_bf[:].rearrange("p (c i t) -> p c t i", i=4, t=PACK),
                in0=silu[hf][:].rearrange("p t (c i) -> p c t i", i=4),
                in1=gain_sb[:].unsqueeze(1).unsqueeze(3).to_broadcast([P, HALF // 4, PACK, 4]),
                op=ALU.mult,
            )
            return h_bf

        h_bf = scale_h(0, "w1_raw2")
        quantize(h_codes[:, :HALF], h_sc[:, :HALF], h_bf[:])
        h_bf = scale_h(1, "w1_bf2")

        v2_words = held("v2_words", [P, S2], U32)
        v2_sc = held("v2_sc", [P, S2], U8)
        nc.vector.tensor_copy(v2_words[:], tab2_sb[:].indirect(offs2_sb[:]))
        quantize(h_codes[:, HALF:], h_sc[:, HALF:], h_bf[:])
        nc.vector.tensor_copy(v2_sc[:], tab2sc_sb[:].indirect(offs2_sb[:]))

        g_banks = [[bank(hf * PACK + t, [P, HALF]) for t in range(PACK)] for hf in range(HALVES)]
        if True:
            for hf in range(HALVES):
                cols = slice(hf * HALF, (hf + 1) * HALF)
                for a in range(PASSES):
                    for t in range(PACK):
                        wcols = slice(t * P, (t + 1) * P)
                        nc.tensor.matmul_mx(
                            out=g_banks[hf][t][:],
                            lhsT=w1_codes[a][:, wcols].bitcast(FP8X4),
                            lhsT_scale=w1_sc[a][:, wcols],
                            rhs=v_words[a][:, cols].bitcast(FP8X4),
                            rhs_scale=v_scales[a][:, cols],
                            start=(a == 0),
                            stop=(a == PASSES - 1),
                        )

        w2_bf = held("w2_bf", [P, PACK * S2], BF16)
        w2_codes = held("w2_codes", [P, S2], U32)
        w2_sc = held("w2_sc", [P, S2], U8)
        nc.scalar.copy(
            out=w2_bf[:].rearrange("p (c i j) -> p c j i", i=4, j=PACK),
            in_=w2_raw[:].rearrange("p j (c i) -> p c j i", i=4),
        )
        quantize(w2_codes[:], w2_sc[:], w2_bf[:])

        g_codes = held("g_codes", [P, S], U32)
        g_sc = held("g_sc", [P, S], U8)
        for hf in range(HALVES):
            g_rows = held("g_rows%d" % hf, [P, PACK, HALF], BF16)
            g_bf = held("g_bf%d" % hf, [P, HALF * PACK], BF16)
            for t in range(PACK):
                nc.scalar.activation(
                    out=g_rows[:, t, :], in_=g_banks[hf][t][:], func=ACT.Identity, bias=b1_sb[:, t : t + 1]
                )
            nc.vector.tensor_copy(
                out=g_bf[:].rearrange("p (c i t) -> p c t i", i=4, t=PACK),
                in_=g_rows[:].rearrange("p t (c i) -> p c t i", i=4),
            )
            cols = slice(hf * HALF, (hf + 1) * HALF)
            quantize(g_codes[:, cols], g_sc[:, cols], g_bf[:])

        e_sb = [held("e%d" % m, [P, S], F32) for m in range(4)]
        match_sb = {}
        for hf in range(HALVES):
            cols = slice(hf * HALF, (hf + 1) * HALF)
            for m in range(4):
                rows = slice(m * P, (m + 1) * P)
                acc = bank(4 + m, [P, HALF])
                nc.tensor.matmul_mx(
                    out=acc[:], lhsT=v2_words[:, rows].bitcast(FP8X4), lhsT_scale=v2_sc[:, rows],
                    rhs=h_codes[:, cols].bitcast(FP8X4), rhs_scale=h_sc[:, cols], start=True, stop=True,
                )
                match_sb[hf, m] = held("match%d_%d" % (hf, m), [P, HALF], F32)
                nc.scalar.copy(out=match_sb[hf, m][:], in_=acc[:])

        def score(hf, m):
            cols = slice(hf * HALF, (hf + 1) * HALF)
            rows = slice(m * P, (m + 1) * P)
            acc = bank(m, [P, HALF])
            nc.tensor.matmul_mx(
                out=acc[:], lhsT=w2_codes[:, rows].bitcast(FP8X4), lhsT_scale=w2_sc[:, rows],
                rhs=g_codes[:, cols].bitcast(FP8X4), rhs_scale=g_sc[:, cols], start=True, stop=True,
            )
            nc.vector.tensor_tensor(out=e_sb[m][:, cols], in0=acc[:], in1=match_sb[hf, m][:], op=ALU.mult)

        for hf in range(HALVES):
            for m in range(4):
                score(hf, m)

        looks, picks = {}, {}

        def fetch(m):
            looks[m] = ring.tile([P, NP], F32, name="look")
            nc.scalar.activation(
                out=looks[m][:], in_=e_sb[m][:].indirect(pos1_sb[:]), func=ACT.Sigmoid,
                bias=thr_sb[:, m : m + 1], scale=sev_sb[:, m : m + 1],
            )
            picks[m] = ring.tile([P, NP], F32, name="pick")
            nc.vector.tensor_tensor(picks[m][:], e_sb[m][:].indirect(pos2_sb[:]), prior_sb[:, m, :], ALU.subtract)

        def finish(m, cols):
            nc.vector.tensor_tensor(out=looks[m][:, cols], in0=looks[m][:, cols], in1=picks[m][:, cols], op=ALU.add)
            nc.sync.dma_start(out=out[m * P : (m + 1) * P, cols], in_=looks[m][:, cols])

        fetch(0)
        for m in range(1, 4):
            fetch(m)
            finish(m - 1, slice(0, NP))
        finish(3, slice(0, NP // 2))
        finish(3, slice(NP // 2, NP))
